import numpy as np
CORES = [97,105,113,121,225,233,241,249,353,361,369,377,481,489,497,505]
N = 16
GROUPS = [[0,4,8,12],[1,5,9,13],[2,6,10,14],[3,7,11,15]]
def setup_inputs(rng):
    return {"x": rng.standard_normal((N, 128, 512), dtype=np.float32)}
def reference(x):
    y = np.empty((N, 128, 512), x.dtype)
    for g in GROUPS:
        n = len(g); b = x.shape[2] // n
        for i, r in enumerate(g):
            y[r] = np.concatenate([x[s][:, i * b:(i + 1) * b] for s in g], axis=1)
    return {"y": y}

@@ -1,0 +1,97 @@
+from concourse.bass import DstId, RemoteDMATransfer
+
+SCRATCH = {
+    "sa": ("dram", [128, 128], "float32"),
+    "sb": ("dram", [128, 128], "float32"),
+    "sc": ("dram", [2, 128, 64], "float32"),
+    "la": ("dram", [128, 128], "float32"),
+    "lb": ("dram", [128, 128], "float32"),
+    "lc": ("dram", [2, 128, 64], "float32"),
+    "hl": ("dram", [128, 64], "float32"),
+}
+SEMAPHORES = ["ldc", "ldab", "sent", "arra", "arrb", "arrc0", "arrc1", "harr", "stored"]
+
+RELAY_CABLE = 2
+RELAY_SWITCH = 4
+
+
+def peers(core, T, topo):
+    rank = T.rank_of(core)
+    grp = [q for q in T.tables["GROUPS"] if rank in q][0]
+    out = {}
+    for j, m in enumerate(grp):
+        d = T.cores[m]
+        if d == core:
+            continue
+        if topo.rack(topo.host(d)) == topo.rack(topo.host(core)):
+            out["rack"] = (j, d)
+        elif topo.may_write(core, d):
+            out["cable"] = (j, d)
+        else:
+            out["diag"] = (j, d)
+    return grp.index(rank), len(grp), out
+
+
+def relays(core, T, topo):
+    p = peers(core, T, topo)[2]
+    return (p["rack"][1] // 8 * 8 + RELAY_CABLE, p["cable"][1] // 8 * 8 + RELAY_SWITCH)
+
+
+def xfer(topo, src_core, dst_core, mask, sem, src, dst):
+    rid, pid = topo.addr(dst_core, src_core)
+    return RemoteDMATransfer(dst_ids=[DstId(rid=rid, pnc=pid)], dma_engine_mask=mask, remote_sem=sem, src=src, dst=dst)
+
+
+def rank_program(g, core, T, topo):
+    S = T.sem
+    if T.rank_of(core) is None:
+        for s in T.cores:
+            rel = relays(s, T, topo)
+            for t in (0, 1):
+                if rel[t] == core:
+                    d = peers(s, T, topo)[2]["diag"][1]
+                    rid, pid = topo.addr(d, core)
+                    g.wait_ge(S.harr, 4)
+                    g.remote_dma(T.lc[t], T.hl[:], S["arrc%d" % t], S.sent, pid, rid, 0xFF)
+                    g.wait_ge(S.sent, 8)
+        return
+
+    i, n, p = peers(core, T, topo)
+    w = T.x.shape[1] // n
+    ja, ca = p["rack"]
+    jb, cb = p["cable"]
+    jc = p["diag"][0]
+    r0, r1 = relays(core, T, topo)
+    sy, sc = g.sync, g.scalar
+
+    def blk(j):
+        return slice(j * w, (j + 1) * w)
+
+    sy.dma_start(T.sc[0], T.x[0:64, blk(jc)]).then_inc(S.ldc, 16)
+    sc.dma_start(T.sc[1], T.x[64:128, blk(jc)]).then_inc(S.ldc, 16)
+    sy.dma_start(T.sa[:], T.x[:, blk(ja)]).then_inc(S.ldab, 16)
+    sc.dma_start(T.sb[:], T.x[:, blk(jb)]).then_inc(S.ldab, 16)
+    sc.dma_start(T.y[:, blk(i)], T.x[:, blk(i)]).then_inc(S.stored, 16)
+
+    g.wait_ge(S.ldc, 32)
+    g.remote_dma_fused([
+        xfer(topo, core, r0, 0x0F, S.harr, T.sc[0], T.hl[:]),
+        xfer(topo, core, r1, 0xF0, S.harr, T.sc[1], T.hl[:]),
+    ], local_sem=S.sent)
+    g.wait_ge(S.ldab, 32)
+    g.remote_dma_fused([
+        xfer(topo, core, ca, 0x0F, S.arra, T.sa[:], T.la[:]),
+        xfer(topo, core, cb, 0xF0, S.arrb, T.sb[:], T.lb[:]),
+    ], local_sem=S.sent)
+
+    sy.wait_ge(S.arra, 4)
+    sy.dma_start(T.y[:, blk(ja)], T.la[:]).then_inc(S.stored, 16)
+    sc.wait_ge(S.arrb, 4)
+    sc.dma_start(T.y[:, blk(jb)], T.lb[:]).then_inc(S.stored, 16)
+    sy.wait_ge(S.arrc0, 8)
+    sy.dma_start(T.y[0:64, blk(jc)], T.lc[0]).then_inc(S.stored, 16)
+    sc.wait_ge(S.arrc1, 8)
+    sc.dma_start(T.y[64:128, blk(jc)], T.lc[1]).then_inc(S.stored, 16)
+
+    g.wait_ge(S.sent, 16)
+    g.wait_ge(S.stored, 80)

@@ -1,18 +1,11 @@
 from concourse.bass import DstId, RemoteDMATransfer
 
 SCRATCH = {
-    "sa": ("dram", [128, 128], "float32"),
-    "sb": ("dram", [128, 128], "float32"),
-    "sc": ("dram", [2, 128, 64], "float32"),
-    "la": ("dram", [128, 128], "float32"),
-    "lb": ("dram", [128, 128], "float32"),
-    "lc": ("dram", [2, 128, 64], "float32"),
+    "st": ("dram", [6, 128, 64], "float32"),
+    "ld": ("dram", [6, 128, 64], "float32"),
     "hl": ("dram", [128, 64], "float32"),
 }
-SEMAPHORES = ["ldc", "ldab", "sent", "arra", "arrb", "arrc0", "arrc1", "harr", "stored"]
-
-RELAY_CABLE = 2
-RELAY_SWITCH = 4
+SEMAPHORES = ["ld1", "ld2", "sent", "ar0", "ar1", "ar2", "ar3", "ar4", "ar5", "harr", "stored"]
 
 
 def peers(core, T, topo):
@@ -34,7 +27,13 @@ def peers(core, T, topo):
 
 def relays(core, T, topo):
     p = peers(core, T, topo)[2]
-    return (p["rack"][1] // 8 * 8 + RELAY_CABLE, p["cable"][1] // 8 * 8 + RELAY_SWITCH)
+    a, b, c = p["rack"][1], p["cable"][1], p["diag"][1]
+    return {
+        0: (a // 8 * 8 + 2, c),
+        1: (b // 8 * 8 + 4, c),
+        3: (core // 8 * 8 + 5, a),
+        5: (core // 8 * 8 + 6, b),
+    }
 
 
 def xfer(topo, src_core, dst_core, mask, sem, src, dst):
@@ -46,13 +45,11 @@ def rank_program(g, core, T, topo):
     S = T.sem
     if T.rank_of(core) is None:
         for s in T.cores:
-            rel = relays(s, T, topo)
-            for t in (0, 1):
-                if rel[t] == core:
-                    d = peers(s, T, topo)[2]["diag"][1]
+            for t, (rc, d) in relays(s, T, topo).items():
+                if rc == core:
                     rid, pid = topo.addr(d, core)
                     g.wait_ge(S.harr, 4)
-                    g.remote_dma(T.lc[t], T.hl[:], S["arrc%d" % t], S.sent, pid, rid, 0xFF)
+                    g.remote_dma(T.ld[t], T.hl[:], S["ar%d" % t], S.sent, pid, rid, 0xFF)
                     g.wait_ge(S.sent, 8)
         return
 
@@ -61,37 +58,35 @@ def rank_program(g, core, T, topo):
     ja, ca = p["rack"]
     jb, cb = p["cable"]
     jc = p["diag"][0]
-    r0, r1 = relays(core, T, topo)
+    rel = relays(core, T, topo)
     sy, sc = g.sync, g.scalar
+    col = {0: jc, 1: jc, 2: ja, 3: ja, 4: jb, 5: jb}
 
-    def blk(j):
-        return slice(j * w, (j + 1) * w)
+    def view(t_, slot):
+        r = 64 * (slot % 2)
+        j = col[slot]
+        return t_[r:r + 64, j * w:(j + 1) * w]
 
-    sy.dma_start(T.sc[0], T.x[0:64, blk(jc)]).then_inc(S.ldc, 16)
-    sc.dma_start(T.sc[1], T.x[64:128, blk(jc)]).then_inc(S.ldc, 16)
-    sy.dma_start(T.sa[:], T.x[:, blk(ja)]).then_inc(S.ldab, 16)
-    sc.dma_start(T.sb[:], T.x[:, blk(jb)]).then_inc(S.ldab, 16)
-    sc.dma_start(T.y[:, blk(i)], T.x[:, blk(i)]).then_inc(S.stored, 16)
+    for q, slot, sem in ((sy, 0, S.ld1), (sc, 1, S.ld1), (sy, 3, S.ld1), (sc, 5, S.ld1), (sy, 2, S.ld2), (sc, 4, S.ld2)):
+        q.dma_start(T.st[slot], view(T.x, slot)).then_inc(sem, 16)
+    sc.dma_start(T.y[:, i * w:(i + 1) * w], T.x[:, i * w:(i + 1) * w]).then_inc(S.stored, 16)
 
-    g.wait_ge(S.ldc, 32)
+    g.wait_ge(S.ld1, 64)
     g.remote_dma_fused([
-        xfer(topo, core, r0, 0x0F, S.harr, T.sc[0], T.hl[:]),
-        xfer(topo, core, r1, 0xF0, S.harr, T.sc[1], T.hl[:]),
+        xfer(topo, core, rel[0][0], 0x000F, S.harr, T.st[0], T.hl[:]),
+        xfer(topo, core, rel[1][0], 0x00F0, S.harr, T.st[1], T.hl[:]),
+        xfer(topo, core, rel[3][0], 0x0F00, S.harr, T.st[3], T.hl[:]),
+        xfer(topo, core, rel[5][0], 0xF000, S.harr, T.st[5], T.hl[:]),
     ], local_sem=S.sent)
-    g.wait_ge(S.ldab, 32)
+    g.wait_ge(S.ld2, 32)
     g.remote_dma_fused([
-        xfer(topo, core, ca, 0x0F, S.arra, T.sa[:], T.la[:]),
-        xfer(topo, core, cb, 0xF0, S.arrb, T.sb[:], T.lb[:]),
+        xfer(topo, core, ca, 0x0F, S.ar2, T.st[2], T.ld[2]),
+        xfer(topo, core, cb, 0xF0, S.ar4, T.st[4], T.ld[4]),
     ], local_sem=S.sent)
 
-    sy.wait_ge(S.arra, 4)
-    sy.dma_start(T.y[:, blk(ja)], T.la[:]).then_inc(S.stored, 16)
-    sc.wait_ge(S.arrb, 4)
-    sc.dma_start(T.y[:, blk(jb)], T.lb[:]).then_inc(S.stored, 16)
-    sy.wait_ge(S.arrc0, 8)
-    sy.dma_start(T.y[0:64, blk(jc)], T.lc[0]).then_inc(S.stored, 16)
-    sc.wait_ge(S.arrc1, 8)
-    sc.dma_start(T.y[64:128, blk(jc)], T.lc[1]).then_inc(S.stored, 16)
+    for q, slot, cnt in ((sy, 2, 4), (sc, 4, 4), (sy, 3, 8), (sc, 5, 8), (sy, 0, 8), (sc, 1, 8)):
+        q.wait_ge(S["ar%d" % slot], cnt)
+        q.dma_start(view(T.y, slot), T.ld[slot]).then_inc(S.stored, 16)
 
-    g.wait_ge(S.sent, 16)
-    g.wait_ge(S.stored, 80)
+    g.wait_ge(S.sent, 24)
+    g.wait_ge(S.stored, 112)

@@ -5,7 +5,8 @@ SCRATCH = {
     "ld": ("dram", [6, 128, 64], "float32"),
     "hl": ("dram", [128, 64], "float32"),
 }
-SEMAPHORES = ["ld1", "ld2", "sent", "ar0", "ar1", "ar2", "ar3", "ar4", "ar5", "harr", "stored"]
+SEMAPHORES = ["ld0", "ld1", "ld2", "sent", "ar0", "ar1", "ar2", "ar3", "ar4", "ar5", "harr", "stored"]
+EARLY_C = True
 
 
 def peers(core, T, topo):
@@ -67,17 +68,21 @@ def rank_program(g, core, T, topo):
         j = col[slot]
         return t_[r:r + 64, j * w:(j + 1) * w]
 
-    for q, slot, sem in ((sy, 0, S.ld1), (sc, 1, S.ld1), (sy, 3, S.ld1), (sc, 5, S.ld1), (sy, 2, S.ld2), (sc, 4, S.ld2)):
+    def relay(slot, mask):
+        return xfer(topo, core, rel[slot][0], mask, S.harr, T.st[slot], T.hl[:])
+
+    for q, slot, sem in ((sy, 0, S.ld0), (sc, 1, S.ld0), (sy, 3, S.ld1), (sc, 5, S.ld1), (sy, 2, S.ld2), (sc, 4, S.ld2)):
         q.dma_start(T.st[slot], view(T.x, slot)).then_inc(sem, 16)
     sc.dma_start(T.y[:, i * w:(i + 1) * w], T.x[:, i * w:(i + 1) * w]).then_inc(S.stored, 16)
 
-    g.wait_ge(S.ld1, 64)
-    g.remote_dma_fused([
-        xfer(topo, core, rel[0][0], 0x000F, S.harr, T.st[0], T.hl[:]),
-        xfer(topo, core, rel[1][0], 0x00F0, S.harr, T.st[1], T.hl[:]),
-        xfer(topo, core, rel[3][0], 0x0F00, S.harr, T.st[3], T.hl[:]),
-        xfer(topo, core, rel[5][0], 0xF000, S.harr, T.st[5], T.hl[:]),
-    ], local_sem=S.sent)
+    g.wait_ge(S.ld0, 32)
+    if EARLY_C:
+        g.remote_dma_fused([relay(0, 0x000F), relay(1, 0x00F0)], local_sem=S.sent)
+        g.wait_ge(S.ld1, 32)
+        g.remote_dma_fused([relay(3, 0x0F00), relay(5, 0xF000)], local_sem=S.sent)
+    else:
+        g.wait_ge(S.ld1, 32)
+        g.remote_dma_fused([relay(0, 0x000F), relay(1, 0x00F0), relay(3, 0x0F00), relay(5, 0xF000)], local_sem=S.sent)
     g.wait_ge(S.ld2, 32)
     g.remote_dma_fused([
         xfer(topo, core, ca, 0x0F, S.ar2, T.st[2], T.ld[2]),

@@ -6,7 +6,6 @@ SCRATCH = {
     "hl": ("dram", [128, 64], "float32"),
 }
 SEMAPHORES = ["ld0", "ld1", "ld2", "sent", "ar0", "ar1", "ar2", "ar3", "ar4", "ar5", "harr", "stored"]
-EARLY_C = True
 
 
 def peers(core, T, topo):
@@ -76,13 +75,9 @@ def rank_program(g, core, T, topo):
     sc.dma_start(T.y[:, i * w:(i + 1) * w], T.x[:, i * w:(i + 1) * w]).then_inc(S.stored, 16)
 
     g.wait_ge(S.ld0, 32)
-    if EARLY_C:
-        g.remote_dma_fused([relay(0, 0x000F), relay(1, 0x00F0)], local_sem=S.sent)
-        g.wait_ge(S.ld1, 32)
-        g.remote_dma_fused([relay(3, 0x0F00), relay(5, 0xF000)], local_sem=S.sent)
-    else:
-        g.wait_ge(S.ld1, 32)
-        g.remote_dma_fused([relay(0, 0x000F), relay(1, 0x00F0), relay(3, 0x0F00), relay(5, 0xF000)], local_sem=S.sent)
+    g.remote_dma_fused([relay(0, 0x000F), relay(1, 0x00F0)], local_sem=S.sent)
+    g.wait_ge(S.ld1, 32)
+    g.remote_dma_fused([relay(3, 0x0F00), relay(5, 0xF000)], local_sem=S.sent)
     g.wait_ge(S.ld2, 32)
     g.remote_dma_fused([
         xfer(topo, core, ca, 0x0F, S.ar2, T.st[2], T.ld[2]),

from concourse.bass import DstId, RemoteDMATransfer

SCRATCH = {
    "st": ("dram", [6, 128, 64], "float32"),
    "ld": ("dram", [6, 128, 64], "float32"),
    "hl": ("dram", [128, 64], "float32"),
}
SEMAPHORES = ["ld0", "ld1", "ld2", "sent", "ar0", "ar1", "ar2", "ar3", "ar4", "ar5", "harr", "stored"]


def peers(core, T, topo):
    rank = T.rank_of(core)
    grp = [q for q in T.tables["GROUPS"] if rank in q][0]
    out = {}
    for j, m in enumerate(grp):
        d = T.cores[m]
        if d == core:
            continue
        if topo.rack(topo.host(d)) == topo.rack(topo.host(core)):
            out["rack"] = (j, d)
        elif topo.may_write(core, d):
            out["cable"] = (j, d)
        else:
            out["diag"] = (j, d)
    return grp.index(rank), len(grp), out


def relays(core, T, topo):
    p = peers(core, T, topo)[2]
    a, b, c = p["rack"][1], p["cable"][1], p["diag"][1]
    return {
        0: (a // 8 * 8 + 2, c),
        1: (b // 8 * 8 + 4, c),
        3: (core // 8 * 8 + 5, a),
        5: (core // 8 * 8 + 6, b),
    }


def xfer(topo, src_core, dst_core, mask, sem, src, dst):
    rid, pid = topo.addr(dst_core, src_core)
    return RemoteDMATransfer(dst_ids=[DstId(rid=rid, pnc=pid)], dma_engine_mask=mask, remote_sem=sem, src=src, dst=dst)


def rank_program(g, core, T, topo):
    S = T.sem
    if T.rank_of(core) is None:
        for s in T.cores:
            for t, (rc, d) in relays(s, T, topo).items():
                if rc == core:
                    rid, pid = topo.addr(d, core)
                    g.wait_ge(S.harr, 4)
                    g.remote_dma(T.ld[t], T.hl[:], S["ar%d" % t], S.sent, pid, rid, 0xFF)
                    g.wait_ge(S.sent, 8)
        return

    i, n, p = peers(core, T, topo)
    w = T.x.shape[1] // n
    ja, ca = p["rack"]
    jb, cb = p["cable"]
    jc = p["diag"][0]
    rel = relays(core, T, topo)
    sy, sc = g.sync, g.scalar
    col = {0: jc, 1: jc, 2: ja, 3: ja, 4: jb, 5: jb}

    def view(t_, slot):
        r = 64 * (slot % 2)
        j = col[slot]
        return t_[r:r + 64, j * w:(j + 1) * w]

    def relay(slot, mask):
        return xfer(topo, core, rel[slot][0], mask, S.harr, T.st[slot], T.hl[:])

    for q, slot, sem in ((sy, 0, S.ld0), (sc, 1, S.ld0), (sy, 3, S.ld1), (sc, 5, S.ld1), (sy, 2, S.ld2), (sc, 4, S.ld2)):
        q.dma_start(T.st[slot], view(T.x, slot)).then_inc(sem, 16)
    sc.dma_start(T.y[:, i * w:(i + 1) * w], T.x[:, i * w:(i + 1) * w]).then_inc(S.stored, 16)

    g.wait_ge(S.ld0, 32)
    g.remote_dma_fused([relay(0, 0x000F), relay(1, 0x00F0)], local_sem=S.sent)
    g.wait_ge(S.ld1, 32)
    g.remote_dma_fused([relay(3, 0x0F00), relay(5, 0xF000)], local_sem=S.sent)
    g.wait_ge(S.ld2, 32)
    g.remote_dma_fused([
        xfer(topo, core, ca, 0x0F, S.ar2, T.st[2], T.ld[2]),
        xfer(topo, core, cb, 0xF0, S.ar4, T.st[4], T.ld[4]),
    ], local_sem=S.sent)

    for q, slot, cnt in ((sy, 2, 4), (sc, 4, 4), (sy, 3, 8), (sc, 5, 8), (sy, 0, 8), (sc, 1, 8)):
        q.wait_ge(S["ar%d" % slot], cnt)
        q.dma_start(view(T.y, slot), T.ld[slot]).then_inc(S.stored, 16)

    g.wait_ge(S.sent, 24)
    g.wait_ge(S.stored, 112)
